import numpy as np
import ml_dtypes


def mxq(x, axis, fmt="e4m3"):
    dtype, down = {"e4m3": (ml_dtypes.float8_e4m3fn, 7), "e5m2": (ml_dtypes.float8_e5m2, 14)}[fmt]
    v = np.moveaxis(np.asarray(x, np.float32).astype(ml_dtypes.bfloat16).astype(np.float64), axis, -1)
    blocks = v.reshape(v.shape[:-1] + (-1, 32))
    amax = np.abs(blocks).max(-1, keepdims=True)
    byte = np.maximum(np.where(amax > 0, np.frexp(amax)[1] - 1 + 127, 0) - down, 1)
    scale = np.exp2(byte - 127.0)
    codes = (blocks / scale).astype(np.float32).astype(dtype).astype(np.float64)
    return np.moveaxis((codes * scale).reshape(v.shape), -1, axis)


WIDE = False


def mx_kscale(k):
    if not WIDE:
        return np.ones(k)
    levels = np.array([10, -10, 5, -5, 0])
    if k % 512:
        return np.exp2(np.random.permutation(np.resize(levels, k // 32))).repeat(32)
    a = np.empty((k // 512, 16))
    for p in range(k // 512):
        a[p, :8] = np.random.permutation(np.resize(levels, 8))
        for g in range(8):
            far = levels[np.abs(levels - a[p, g]) >= 10]
            a[p, g + 8] = far[np.random.randint(len(far))]
    return np.exp2(a.ravel()).repeat(32)


BF16 = ml_dtypes.bfloat16


def bf(x):
    return np.asarray(x, np.float32).astype(BF16)


def f64(x):
    return np.asarray(x).astype(np.float64)


T, D, F, R = 1024, 1024, 1024, 512


def draw0():
    kd, kt = mx_kscale(D), mx_kscale(T)
    return {"x": bf(np.random.standard_normal((T, D)) * kd),
            "wm": bf(np.random.standard_normal((D, F)) / np.sqrt(D) / kd[:, None]),
            "a": bf(np.random.standard_normal((D, R)) / np.sqrt(D) / kd[:, None]),
            "target": bf(np.random.standard_normal((T, F))),
            "s": bf((1.0 + 0.25 * np.random.standard_normal(T)) / kt),
            "wt": bf(np.random.uniform(0.5, 1.5, T) * kt)}


def scale_tokens(gain, rows):
    return gain[:, None] * rows


def core(x, wm, a, target, s, wt):
    root_t = np.sqrt(T)
    xq = mxq(f64(x), 1, "e4m3")
    u = xq @ mxq(f64(a), 0, "e4m3")
    y = xq @ mxq(f64(wm), 0, "e4m3")
    ug = scale_tokens(f64(s), u)
    e = scale_tokens(f64(wt), np.tanh(y - f64(target)))
    return (mxq(ug.T, 1, "e4m3") @ mxq(e, 0, "e4m3")) / root_t


def e4m3fn_bytes(y):
    return np.clip(np.asarray(y, np.float64), -448.0, 448.0).astype(np.float32).astype(ml_dtypes.float8_e4m3fn).view(np.uint8)


def e4m3fn_values(b):
    return np.asarray(b, np.uint8).view(ml_dtypes.float8_e4m3fn).astype(np.float64)


def setup_inputs():
    d = draw0()
    x0 = np.asarray(d['x']).astype(np.float64)
    s = (np.max(np.abs(x0), axis=(0,), keepdims=True) / 448.0).astype(np.float32)
    out = {}
    for k, v in d.items():
        if k == 'x':
            out['x_bytes'] = e4m3fn_bytes(x0 / s.astype(np.float64))
            out['x_scale'] = s
        else:
            out[k] = v
    return out


def reference(x_bytes, x_scale, wm, a, target, s, wt):
    return core(e4m3fn_values(x_bytes) * x_scale.astype(np.float64), wm, a, target, s, wt)

@@ -1,0 +1,340 @@
+from contextlib import ExitStack
+
+import concourse.mybir as mybir
+from concourse.masks import make_identity
+
+T, D, F, R = 1024, 1024, 1024, 512
+P = 128
+J = 4
+KP = P * J
+H = T // KP
+G = D // KP
+NF = 512
+FH = F // NF
+
+FLOPS = 2 * T * D * F + 2 * T * D * R + 2 * T * R * F
+
+F32 = mybir.dt.float32
+BF16 = mybir.dt.bfloat16
+U32 = mybir.dt.uint32
+U8 = mybir.dt.uint8
+FP8 = mybir.dt.float8_e4m3fn
+FP8X4 = mybir.dt.float8_e4m3fn_x4
+ALU = mybir.AluOpType
+ACT = mybir.ActivationFunctionType
+
+
+def tile_lorafalogcoshgradient_kernel(tc, x_bytes, x_scale, wm, a, target, s, wt, out):
+    nc = tc.nc
+    with ExitStack() as ctx:
+        keep = ctx.enter_context(tc.tile_pool(name="keep", bufs=1))
+        psum = ctx.enter_context(tc.psum_pool(name="psum", bufs=1))
+        ctx.enter_context(tc.manual_schedule())
+
+        def sb(name, shape, dt):
+            return keep.tile(shape, dt, name=name, align_bytes=64)
+
+        xs_sb = sb("xs_sb", [P, G, J], F32)
+        s_bf = sb("s_bf", [P, H, J], BF16)
+        wt_bf = sb("wt_bf", [P, H, J], BF16)
+        s32 = sb("s32", [P, H, J], F32)
+        wt32 = sb("wt32", [P, H, J], F32)
+        xb = [sb(f"xb{h}", [P, J, D], U8) for h in range(H)]
+        wraw = [[sb(f"wraw{f}_{g}", [P, J, NF], BF16) for g in range(G)] for f in range(FH)]
+        araw = [sb(f"araw{g}", [P, J, R], BF16) for g in range(G)]
+        traw = [[sb(f"traw{h}_{f}", [P, J, NF], BF16) for f in range(FH)] for h in range(H)]
+
+        x_v = x_bytes.rearrange("(h p j) d -> h p j d", p=P, j=J)
+        wm_v = wm.rearrange("(g p j) f -> g p j f", p=P, j=J)
+        a_v = a.rearrange("(g p j) r -> g p j r", p=P, j=J)
+        t_v = target.rearrange("(h p j) f -> h p j f", p=P, j=J)
+
+        def load_x(h, j0, n):
+            nc.sync.dma_start(out=xb[h][:, j0 : j0 + n, :], in_=x_v[h][:, j0 : j0 + n, :])
+
+        def load_w(f, g):
+            nc.sync.dma_start(out=wraw[f][g][:], in_=wm_v[g][:, :, f * NF : (f + 1) * NF])
+
+        def load_t(h, f):
+            nc.sync.dma_start(out=traw[h][f][:], in_=t_v[h][:, :, f * NF : (f + 1) * NF])
+
+        nc.scalar.dma_start(out=xs_sb[:], in_=x_scale.rearrange("o (g p t) -> p (o g) t", p=P, t=J))
+        for j in range(J):
+            load_x(0, j, 1)
+        load_x(1, 0, 2)
+        load_w(0, 0)
+        load_x(1, 2, 2)
+        load_w(0, 1)
+        nc.scalar.dma_start(out=wt_bf[:], in_=wt.rearrange("(h p j) -> p h j", p=P, j=J))
+        nc.scalar.dma_start(out=s_bf[:], in_=s.rearrange("(h p j) -> p h j", p=P, j=J))
+        for g in range(G):
+            nc.sync.dma_start(out=araw[g][:], in_=a_v[g])
+        load_t(0, 0)
+        load_t(1, 0)
+        load_w(1, 0)
+        load_w(1, 1)
+        load_t(0, 1)
+        load_t(1, 1)
+
+        warm = sb("warm", [P, 1], F32)
+        warm_o = sb("warm_o", [P, 1], F32)
+        nc.vector.memset(warm[:], 0.0)
+        nc.scalar.activation(warm_o[:], warm[:], ACT.Tanh)
+        id32 = sb("id32", [P, P], F32)
+        make_identity(nc, id32[:])
+        idb = sb("idb", [P, P], BF16)
+        make_identity(nc, idb[:])
+
+        xcast = [[sb(f"xcast{h}_{sp}", [P, 2, D], BF16) for sp in range(2)] for h in range(H)]
+        xg = [[sb(f"xg{h}_{g}", [P, KP, J], BF16) for g in range(G)] for h in range(H)]
+        xq = [[sb(f"xq{h}_{g}", [P, KP], U32) for g in range(G)] for h in range(H)]
+        xsc = [[sb(f"xsc{h}_{g}", [P, KP], U8) for g in range(G)] for h in range(H)]
+        wg = [[sb(f"wg{f}_{g}", [P, NF, J], BF16) for g in range(G)] for f in range(FH)]
+        wq = [[sb(f"wq{f}_{g}", [P, NF], U32) for g in range(G)] for f in range(FH)]
+        wsc = [[sb(f"wsc{f}_{g}", [P, NF], U8) for g in range(G)] for f in range(FH)]
+        ag = [sb(f"ag{g}", [P, R, J], BF16) for g in range(G)]
+        aq = [sb(f"aq{g}", [P, R], U32) for g in range(G)]
+        asc = [sb(f"asc{g}", [P, R], U8) for g in range(G)]
+        up = [sb(f"up{h}", [P, J, R], BF16) for h in range(H)]
+        ug = [sb(f"ug{h}", [P, R, J], BF16) for h in range(H)]
+        uq = [sb(f"uq{h}", [P, R], U32) for h in range(H)]
+        usc = [sb(f"usc{h}", [P, R], U8) for h in range(H)]
+        eq = [sb(f"eq{h}", [P, F], U32) for h in range(H)]
+        esc = [sb(f"esc{h}", [P, F], U8) for h in range(H)]
+
+        def tp(shape, dt):
+            return psum.tile(shape, dt, name="tp", bufs=3)
+
+        def acc(shape):
+            return psum.tile(shape, F32, name="acc", bufs=5)
+
+        def quant(codes, scales, src):
+            nc.vector.quantize_mx(out=codes.bitcast(FP8X4), scales=scales, in_=src)
+
+        def flat(t):
+            return t.rearrange("p n j -> p (n j)")
+
+        def mx(o, lq, ls, rq, rs, start, stop):
+            nc.tensor.matmul_mx(
+                out=o, lhsT=lq.bitcast(FP8X4), lhsT_scale=ls, rhs=rq.bitcast(FP8X4), rhs_scale=rs, start=start, stop=stop
+            )
+
+        def cast(h, j, eng):
+            src = xb[h][:, j, :].bitcast(FP8)
+            dst = xcast[h][j // 2][:, j % 2, :]
+            if eng == "V":
+                nc.vector.tensor_copy(dst, src)
+            else:
+                nc.scalar.copy(dst, src)
+
+        def words(h, j, g, u):
+            w = xcast[h][j // 2][:, j % 2, :].bitcast(F32)
+            lo = g * 2 * P + u
+            return w[:, lo : lo + 2 * P - 1 : 2]
+
+        def x_exit(h, g, bank_view, n0, n):
+            xin = bank_view.rearrange("p u n -> p (u n)").bitcast(BF16).rearrange("p (u n e) -> p n u e", u=2, e=2)
+            dst = xg[h][g][:, n0 : n0 + n, :].rearrange("p n (u e) -> p n u e", u=2)
+            sc = xs_sb[:, g, :].rearrange("p (u e) -> p u e", u=2).unsqueeze(1).to_broadcast([P, n, 2, 2])
+            nc.vector.tensor_tensor(dst, xin, sc, ALU.mult)
+
+        def turn1(h, j):
+            bank = tp([P, G, 2, P], F32)
+            for g in range(G):
+                for u in range(2):
+                    nc.tensor.transpose(bank[:, g, u, :], words(h, j, g, u), id32[:])
+            return bank
+
+        def xe1(h, j, bank):
+            for g in range(G):
+                x_exit(h, g, bank[:, g, :, :], j * P, P)
+
+        def turn(h, sp):
+            banks = []
+            for g in range(G):
+                bank = tp([P, 2, 2 * P], F32)
+                for j in range(2):
+                    for u in range(2):
+                        nc.tensor.transpose(bank[:, u, j * P : (j + 1) * P], words(h, 2 * sp + j, g, u), id32[:])
+                banks.append(bank)
+            return banks
+
+        def xe(h, sp, banks):
+            for g in range(G):
+                x_exit(h, g, banks[g][:], 2 * P * sp, 2 * P)
+
+        def x_quant(h):
+            for g in range(G):
+                quant(xq[h][g][:], xsc[h][g][:], flat(xg[h][g][:]))
+
+        def il(dst, raw, c):
+            bank = tp([P, 256, J], BF16)
+            for q in range(2):
+                lo = c * 256 + q * P
+                nc.tensor.matmul(
+                    bank[:, q * P : (q + 1) * P, :],
+                    lhsT=idb[:],
+                    rhs=raw[:, :, lo : lo + P].rearrange("p j n -> p n j"),
+                    start=True,
+                    stop=True,
+                )
+            nc.scalar.copy(dst[:, c * 256 : (c + 1) * 256, :], bank[:])
+
+        def il_g(dst, raw):
+            for c in range(4):
+                cs = slice(c * P, (c + 1) * P)
+                nc.gpsimd.tensor_scalar(
+                    dst[:, cs, :], raw[:, :, cs].rearrange("p j n -> p n j"), 1.0, 0.0, ALU.mult, ALU.add
+                )
+
+        def w_quant(f, g):
+            quant(wq[f][g][:], wsc[f][g][:], flat(wg[f][g][:]))
+
+        def a_quant(g):
+            quant(aq[g][:], asc[g][:], flat(ag[g][:]))
+
+        def u(h):
+            for j in range(J):
+                bank = acc([P, R])
+                ms = slice(j * P, (j + 1) * P)
+                for g in range(G):
+                    mx(bank[:], xq[h][g][:, ms], xsc[h][g][:, ms], aq[g][:], asc[g][:], g == 0, g == G - 1)
+                nc.scalar.activation(up[h][:, j, :], bank[:], ACT.Copy, scale=s32[:, h, j : j + 1])
+
+        def u_quant(h):
+            quant(uq[h][:], usc[h][:], flat(ug[h][:]))
+
+        def y(h, f):
+            z = sb(f"z{h}", [P, J, NF], F32)
+            for j in range(J):
+                bank = acc([P, NF])
+                ms = slice(j * P, (j + 1) * P)
+                for g in range(G):
+                    mx(bank[:], xq[h][g][:, ms], xsc[h][g][:, ms], wq[f][g][:], wsc[f][g][:], g == 0, g == G - 1)
+                nc.vector.tensor_tensor(z[:, j, :], bank[:], traw[h][f][:, j, :], ALU.subtract)
+            return z
+
+        def tanh_planes(h, z):
+            th = sb(f"th{h}", [P, J, NF], F32)
+            for k in range(2):
+                nc.scalar.activation(th[:, 2 * k : 2 * k + 2, :], z[:, 2 * k : 2 * k + 2, :], ACT.Tanh)
+            return th
+
+        def tanh_mixed(h, z):
+            th = sb(f"th{h}", [P, NF, J], F32)
+            for k in range(2):
+                cs = slice(k * 256, (k + 1) * 256)
+                nc.scalar.activation(th[:, cs, :], z[:, :, cs].rearrange("p j n -> p n j"), ACT.Tanh)
+            return th
+
+        def wt_planes(h, th):
+            ep = sb(f"ep{h}", [P, J, NF], BF16)
+            for j in range(J):
+                nc.vector.tensor_scalar(ep[:, j, :], th[:, j, :], wt32[:, h, j : j + 1], None, ALU.mult)
+            return ep
+
+        def wt_mixed(h, th, eg, k):
+            cs = slice(k * 256, (k + 1) * 256)
+            nc.vector.tensor_tensor(
+                eg[:, cs, :], th[:, cs, :], wt32[:, h, :].unsqueeze(1).to_broadcast([P, 256, J]), ALU.mult
+            )
+
+        def e_quant(h, f, eg, k):
+            cs = slice(f * NF + k * 256, f * NF + (k + 1) * 256)
+            quant(eq[h][:, cs], esc[h][:, cs], flat(eg[:, k * 256 : (k + 1) * 256, :]))
+
+        def o(f, m, c0, n, eng, tag):
+            bank = tp([P, n], F32) if tag == "tp" else acc([P, n])
+            ms = slice(m * P, (m + 1) * P)
+            cs = slice(f * NF + c0, f * NF + c0 + n)
+            for h in range(H):
+                mx(bank[:], uq[h][:, ms], usc[h][:, ms], eq[h][:, cs], esc[h][:, cs], h == 0, h == H - 1)
+            res = sb(f"res{m}_{c0}_{n}", [P, n], F32)
+            if eng == "V":
+                nc.vector.tensor_scalar(res[:], bank[:], 1.0 / 32.0, None, ALU.mult)
+            else:
+                nc.scalar.activation(res[:], bank[:], ACT.Copy, scale=1.0 / 32.0)
+            nc.sync.dma_start(out=out[ms, cs], in_=res[:])
+
+        def new_eg(h):
+            return sb(f"eg{h}", [P, NF, J], BF16)
+
+        cast(0, 0, "V")
+        cast(0, 1, "S")
+        cast(0, 2, "V")
+        cast(0, 3, "S")
+        b = turn1(0, 0)
+        xe1(0, 0, b)
+        b = turn1(0, 1)
+        xe1(0, 1, b)
+        b = turn(0, 1)
+        cast(1, 0, "S")
+        cast(1, 1, "S")
+        xe(0, 1, b)
+        nc.vector.tensor_copy(wt32[:], wt_bf[:])
+        nc.vector.tensor_copy(s32[:], s_bf[:])
+        for c in range(2):
+            il(wg[0][0], wraw[0][0], c)
+        b = turn(1, 0)
+        x_quant(0)
+        cast(1, 2, "S")
+        cast(1, 3, "S")
+        xe(1, 0, b)
+        for c in range(2):
+            il(wg[0][1], wraw[0][1], c)
+        b = turn(1, 1)
+        for g in range(G):
+            il_g(ag[g], araw[g])
+        w_quant(0, 0)
+        w_quant(0, 1)
+        z00 = y(0, 0)
+        th00 = tanh_planes(0, z00)
+        a_quant(0)
+        a_quant(1)
+        u(0)
+        xe(1, 1, b)
+        x_quant(1)
+        for g in range(G):
+            il_g(wg[1][g], wraw[1][g])
+        z10 = y(1, 0)
+        for c in range(2):
+            il(ug[0], up[0], c)
+        ep00 = wt_planes(0, th00)
+        u(1)
+        th10 = tanh_planes(1, z10)
+        w_quant(1, 0)
+        w_quant(1, 1)
+        u_quant(0)
+        eg00 = new_eg(0)
+        for c in range(2):
+            il(eg00, ep00, c)
+        ep10 = wt_planes(1, th10)
+        z01 = y(0, 1)
+        for c in range(2):
+            il(ug[1], up[1], c)
+        for k in range(2):
+            e_quant(0, 0, eg00, k)
+        th01 = tanh_mixed(0, z01)
+        z11 = y(1, 1)
+        eg10 = new_eg(1)
+        for c in range(2):
+            il(eg10, ep10, c)
+        u_quant(1)
+        for k in range(2):
+            e_quant(1, 0, eg10, k)
+        th11 = tanh_mixed(1, z11)
+        eg01 = new_eg(0)
+        for k in range(2):
+            wt_mixed(0, th01, eg01, k)
+        for m in range(4):
+            o(0, m, 0, NF, "S", "acc")
+        for k in range(2):
+            e_quant(0, 1, eg01, k)
+        eg11 = new_eg(1)
+        for k in range(2):
+            wt_mixed(1, th11, eg11, k)
+        for k in range(2):
+            e_quant(1, 1, eg11, k)
+        for k in range(2):
+            for m in range(4):
+                o(1, m, k * 256, 256, "VS"[m % 2], "tp")

@@ -42,39 +42,35 @@ def tile_lorafalogcoshgradient_kernel(tc, x_bytes, x_scale, wm, a, target, s, wt
         xb = [sb(f"xb{h}", [P, J, D], U8) for h in range(H)]
         wraw = [[sb(f"wraw{f}_{g}", [P, J, NF], BF16) for g in range(G)] for f in range(FH)]
         araw = [sb(f"araw{g}", [P, J, R], BF16) for g in range(G)]
-        traw = [[sb(f"traw{h}_{f}", [P, J, NF], BF16) for f in range(FH)] for h in range(H)]
+        traw = [sb(f"traw{h}", [P, J, F], BF16) for h in range(H)]
 
         x_v = x_bytes.rearrange("(h p j) d -> h p j d", p=P, j=J)
         wm_v = wm.rearrange("(g p j) f -> g p j f", p=P, j=J)
         a_v = a.rearrange("(g p j) r -> g p j r", p=P, j=J)
         t_v = target.rearrange("(h p j) f -> h p j f", p=P, j=J)
 
-        def load_x(h, j0, n):
-            nc.sync.dma_start(out=xb[h][:, j0 : j0 + n, :], in_=x_v[h][:, j0 : j0 + n, :])
+        def load_x(h, sp):
+            js = slice(2 * sp, 2 * sp + 2)
+            nc.sync.dma_start(out=xb[h][:, js, :], in_=x_v[h][:, js, :])
 
         def load_w(f, g):
             nc.sync.dma_start(out=wraw[f][g][:], in_=wm_v[g][:, :, f * NF : (f + 1) * NF])
 
-        def load_t(h, f):
-            nc.sync.dma_start(out=traw[h][f][:], in_=t_v[h][:, :, f * NF : (f + 1) * NF])
-
         nc.scalar.dma_start(out=xs_sb[:], in_=x_scale.rearrange("o (g p t) -> p (o g) t", p=P, t=J))
-        for j in range(J):
-            load_x(0, j, 1)
-        load_x(1, 0, 2)
+        load_x(0, 0)
+        load_x(0, 1)
+        load_x(1, 0)
         load_w(0, 0)
-        load_x(1, 2, 2)
+        load_x(1, 1)
         load_w(0, 1)
         nc.scalar.dma_start(out=wt_bf[:], in_=wt.rearrange("(h p j) -> p h j", p=P, j=J))
         nc.scalar.dma_start(out=s_bf[:], in_=s.rearrange("(h p j) -> p h j", p=P, j=J))
         for g in range(G):
             nc.sync.dma_start(out=araw[g][:], in_=a_v[g])
-        load_t(0, 0)
-        load_t(1, 0)
+        nc.sync.dma_start(out=traw[0][:], in_=t_v[0])
         load_w(1, 0)
         load_w(1, 1)
-        load_t(0, 1)
-        load_t(1, 1)
+        nc.sync.dma_start(out=traw[1][:], in_=t_v[1])
 
         warm = sb("warm", [P, 1], F32)
         warm_o = sb("warm_o", [P, 1], F32)
@@ -82,8 +78,6 @@ def tile_lorafalogcoshgradient_kernel(tc, x_bytes, x_scale, wm, a, target, s, wt
         nc.scalar.activation(warm_o[:], warm[:], ACT.Tanh)
         id32 = sb("id32", [P, P], F32)
         make_identity(nc, id32[:])
-        idb = sb("idb", [P, P], BF16)
-        make_identity(nc, idb[:])
 
         xcast = [[sb(f"xcast{h}_{sp}", [P, 2, D], BF16) for sp in range(2)] for h in range(H)]
         xg = [[sb(f"xg{h}_{g}", [P, KP, J], BF16) for g in range(G)] for h in range(H)]
@@ -99,20 +93,18 @@ def tile_lorafalogcoshgradient_kernel(tc, x_bytes, x_scale, wm, a, target, s, wt
         ug = [sb(f"ug{h}", [P, R, J], BF16) for h in range(H)]
         uq = [sb(f"uq{h}", [P, R], U32) for h in range(H)]
         usc = [sb(f"usc{h}", [P, R], U8) for h in range(H)]
+        eg = [[sb(f"eg{h}_{f}", [P, NF, J], BF16) for f in range(FH)] for h in range(H)]
         eq = [sb(f"eq{h}", [P, F], U32) for h in range(H)]
         esc = [sb(f"esc{h}", [P, F], U8) for h in range(H)]
 
-        def tp(shape, dt):
-            return psum.tile(shape, dt, name="tp", bufs=3)
+        def tp(shape):
+            return psum.tile(shape, F32, name="tp", bufs=3)
 
         def acc(shape):
             return psum.tile(shape, F32, name="acc", bufs=5)
 
         def quant(codes, scales, src):
-            nc.vector.quantize_mx(out=codes.bitcast(FP8X4), scales=scales, in_=src)
-
-        def flat(t):
-            return t.rearrange("p n j -> p (n j)")
+            nc.vector.quantize_mx(out=codes.bitcast(FP8X4), scales=scales, in_=src.rearrange("p n j -> p (n j)"))
 
         def mx(o, lq, ls, rq, rs, start, stop):
             nc.tensor.matmul_mx(
@@ -139,7 +131,7 @@ def tile_lorafalogcoshgradient_kernel(tc, x_bytes, x_scale, wm, a, target, s, wt
             nc.vector.tensor_tensor(dst, xin, sc, ALU.mult)
 
         def turn1(h, j):
-            bank = tp([P, G, 2, P], F32)
+            bank = tp([P, G, 2, P])
             for g in range(G):
                 for u in range(2):
                     nc.tensor.transpose(bank[:, g, u, :], words(h, j, g, u), id32[:])
@@ -149,115 +141,105 @@ def tile_lorafalogcoshgradient_kernel(tc, x_bytes, x_scale, wm, a, target, s, wt
             for g in range(G):
                 x_exit(h, g, bank[:, g, :, :], j * P, P)
 
-        def turn(h, sp):
-            banks = []
-            for g in range(G):
-                bank = tp([P, 2, 2 * P], F32)
-                for j in range(2):
-                    for u in range(2):
-                        nc.tensor.transpose(bank[:, u, j * P : (j + 1) * P], words(h, 2 * sp + j, g, u), id32[:])
-                banks.append(bank)
-            return banks
+        def turn2(h, sp, g):
+            bank = tp([P, 2, 2 * P])
+            for j in range(2):
+                for u in range(2):
+                    nc.tensor.transpose(bank[:, u, j * P : (j + 1) * P], words(h, 2 * sp + j, g, u), id32[:])
+            return bank
 
-        def xe(h, sp, banks):
-            for g in range(G):
-                x_exit(h, g, banks[g][:], 2 * P * sp, 2 * P)
+        def xe2(h, sp, g, bank):
+            x_exit(h, g, bank[:], 2 * P * sp, 2 * P)
 
         def x_quant(h):
             for g in range(G):
-                quant(xq[h][g][:], xsc[h][g][:], flat(xg[h][g][:]))
+                quant(xq[h][g][:], xsc[h][g][:], xg[h][g][:])
 
-        def il(dst, raw, c):
-            bank = tp([P, 256, J], BF16)
-            for q in range(2):
-                lo = c * 256 + q * P
-                nc.tensor.matmul(
-                    bank[:, q * P : (q + 1) * P, :],
-                    lhsT=idb[:],
-                    rhs=raw[:, :, lo : lo + P].rearrange("p j n -> p n j"),
-                    start=True,
-                    stop=True,
-                )
-            nc.scalar.copy(dst[:, c * 256 : (c + 1) * 256, :], bank[:])
+        def half(c):
+            return slice(c * 256, (c + 1) * 256)
 
-        def il_g(dst, raw):
+        def by4(dst, src):
+            return (
+                dst.rearrange("p (c i) t -> p c t i", i=4),
+                src.rearrange("p t (c i) -> p c t i", i=4),
+            )
+
+        def mix_s(dst, src, c):
+            d, q = by4(dst[:, half(c), :], src[:, :, half(c)])
+            nc.scalar.copy(d, q)
+
+        def mix_v(dst, src, c):
+            d, q = by4(dst[:, half(c), :], src[:, :, half(c)])
+            nc.vector.tensor_copy(d, q)
+
+        def mix_g(dst, src):
             for c in range(4):
                 cs = slice(c * P, (c + 1) * P)
                 nc.gpsimd.tensor_scalar(
-                    dst[:, cs, :], raw[:, :, cs].rearrange("p j n -> p n j"), 1.0, 0.0, ALU.mult, ALU.add
+                    dst[:, cs, :], src[:, :, cs].rearrange("p j n -> p n j"), 1.0, 0.0, ALU.mult, ALU.add
                 )
 
         def w_quant(f, g):
-            quant(wq[f][g][:], wsc[f][g][:], flat(wg[f][g][:]))
+            quant(wq[f][g][:], wsc[f][g][:], wg[f][g][:])
 
         def a_quant(g):
-            quant(aq[g][:], asc[g][:], flat(ag[g][:]))
+            quant(aq[g][:], asc[g][:], ag[g][:])
 
-        def u(h):
-            for j in range(J):
-                bank = acc([P, R])
-                ms = slice(j * P, (j + 1) * P)
-                for g in range(G):
-                    mx(bank[:], xq[h][g][:, ms], xsc[h][g][:, ms], aq[g][:], asc[g][:], g == 0, g == G - 1)
-                nc.scalar.activation(up[h][:, j, :], bank[:], ACT.Copy, scale=s32[:, h, j : j + 1])
+        def u(h, j):
+            bank = acc([P, R])
+            ms = slice(j * P, (j + 1) * P)
+            for g in range(G):
+                mx(bank[:], xq[h][g][:, ms], xsc[h][g][:, ms], aq[g][:], asc[g][:], g == 0, g == G - 1)
+            nc.scalar.activation(up[h][:, j, :], bank[:], ACT.Copy, scale=s32[:, h, j : j + 1])
 
         def u_quant(h):
-            quant(uq[h][:], usc[h][:], flat(ug[h][:]))
+            quant(uq[h][:], usc[h][:], ug[h][:])
 
-        def y(h, f):
-            z = sb(f"z{h}", [P, J, NF], F32)
-            for j in range(J):
-                bank = acc([P, NF])
-                ms = slice(j * P, (j + 1) * P)
-                for g in range(G):
-                    mx(bank[:], xq[h][g][:, ms], xsc[h][g][:, ms], wq[f][g][:], wsc[f][g][:], g == 0, g == G - 1)
-                nc.vector.tensor_tensor(z[:, j, :], bank[:], traw[h][f][:, j, :], ALU.subtract)
-            return z
+        def new_z(h):
+            return sb(f"z{h}", [P, J, NF], F32)
 
-        def tanh_planes(h, z):
-            th = sb(f"th{h}", [P, J, NF], F32)
-            for k in range(2):
-                nc.scalar.activation(th[:, 2 * k : 2 * k + 2, :], z[:, 2 * k : 2 * k + 2, :], ACT.Tanh)
-            return th
+        def new_th(h):
+            return sb(f"th{h}", [P, NF, J], F32)
 
-        def tanh_mixed(h, z):
-            th = sb(f"th{h}", [P, NF, J], F32)
-            for k in range(2):
-                cs = slice(k * 256, (k + 1) * 256)
-                nc.scalar.activation(th[:, cs, :], z[:, :, cs].rearrange("p j n -> p n j"), ACT.Tanh)
-            return th
+        def y(h, f, j, z):
+            bank = acc([P, NF])
+            ms = slice(j * P, (j + 1) * P)
+            for g in range(G):
+                mx(bank[:], xq[h][g][:, ms], xsc[h][g][:, ms], wq[f][g][:], wsc[f][g][:], g == 0, g == G - 1)
+            nc.vector.tensor_tensor(z[:, j, :], bank[:], traw[h][:, j, f * NF : (f + 1) * NF], ALU.subtract)
 
-        def wt_planes(h, th):
-            ep = sb(f"ep{h}", [P, J, NF], BF16)
-            for j in range(J):
-                nc.vector.tensor_scalar(ep[:, j, :], th[:, j, :], wt32[:, h, j : j + 1], None, ALU.mult)
-            return ep
+        def tanh(z, th, k):
+            nc.scalar.activation(th[:, half(k), :], z[:, :, half(k)].rearrange("p j n -> p n j"), ACT.Tanh)
 
-        def wt_mixed(h, th, eg, k):
-            cs = slice(k * 256, (k + 1) * 256)
-            nc.vector.tensor_tensor(
-                eg[:, cs, :], th[:, cs, :], wt32[:, h, :].unsqueeze(1).to_broadcast([P, 256, J]), ALU.mult
+        def weigh(eng, h, f, th, c0, n):
+            cs = slice(c0, c0 + n)
+            eng.tensor_tensor(
+                eg[h][f][:, cs, :], th[:, cs, :], wt32[:, h, :].unsqueeze(1).to_broadcast([P, n, J]), ALU.mult
             )
 
-        def e_quant(h, f, eg, k):
-            cs = slice(f * NF + k * 256, f * NF + (k + 1) * 256)
-            quant(eq[h][:, cs], esc[h][:, cs], flat(eg[:, k * 256 : (k + 1) * 256, :]))
+        def weigh_v(h, f, th, k):
+            weigh(nc.vector, h, f, th, k * 256, 256)
 
-        def o(f, m, c0, n, eng, tag):
-            bank = tp([P, n], F32) if tag == "tp" else acc([P, n])
+        def weigh_g(h, f, th, k):
+            for q in range(2):
+                weigh(nc.gpsimd, h, f, th, k * 256 + q * P, P)
+
+        def e_quant(h, f, k):
+            cs = slice(f * NF + k * 256, f * NF + (k + 1) * 256)
+            quant(eq[h][:, cs], esc[h][:, cs], eg[h][f][:, half(k), :])
+
+        def o_pass(bank, h, m, c0, n):
             ms = slice(m * P, (m + 1) * P)
-            cs = slice(f * NF + c0, f * NF + c0 + n)
-            for h in range(H):
-                mx(bank[:], uq[h][:, ms], usc[h][:, ms], eq[h][:, cs], esc[h][:, cs], h == 0, h == H - 1)
-            res = sb(f"res{m}_{c0}_{n}", [P, n], F32)
+            cs = slice(c0, c0 + n)
+            mx(bank[:], uq[h][:, ms], usc[h][:, ms], eq[h][:, cs], esc[h][:, cs], h == 0, h == H - 1)
+
+        def o_store(bank, m, c0, n, eng):
+            res = sb(f"res{m}_{c0}", [P, n], F32)
             if eng == "V":
                 nc.vector.tensor_scalar(res[:], bank[:], 1.0 / 32.0, None, ALU.mult)
             else:
                 nc.scalar.activation(res[:], bank[:], ACT.Copy, scale=1.0 / 32.0)
-            nc.sync.dma_start(out=out[ms, cs], in_=res[:])
-
-        def new_eg(h):
-            return sb(f"eg{h}", [P, NF, J], BF16)
+            nc.sync.dma_start(out=out[m * P : (m + 1) * P, c0 : c0 + n], in_=res[:])
 
         cast(0, 0, "V")
         cast(0, 1, "S")
@@ -267,74 +249,109 @@ def tile_lorafalogcoshgradient_kernel(tc, x_bytes, x_scale, wm, a, target, s, wt
         xe1(0, 0, b)
         b = turn1(0, 1)
         xe1(0, 1, b)
-        b = turn(0, 1)
+        b0 = turn2(0, 1, 0)
+        b1 = turn2(0, 1, 1)
         cast(1, 0, "S")
         cast(1, 1, "S")
-        xe(0, 1, b)
+        xe2(0, 1, 0, b0)
+        xe2(0, 1, 1, b1)
+        for c in range(2):
+            for g in range(G):
+                mix_s(wg[0][g], wraw[0][g], c)
         nc.vector.tensor_copy(wt32[:], wt_bf[:])
         nc.vector.tensor_copy(s32[:], s_bf[:])
-        for c in range(2):
-            il(wg[0][0], wraw[0][0], c)
-        b = turn(1, 0)
+        for g in range(G):
+            mix_g(ag[g], araw[g])
+        b0 = turn2(1, 0, 0)
+        b1 = turn2(1, 0, 1)
         x_quant(0)
+        xe2(1, 0, 0, b0)
         cast(1, 2, "S")
         cast(1, 3, "S")
-        xe(1, 0, b)
-        for c in range(2):
-            il(wg[0][1], wraw[0][1], c)
-        b = turn(1, 1)
-        for g in range(G):
-            il_g(ag[g], araw[g])
         w_quant(0, 0)
         w_quant(0, 1)
-        z00 = y(0, 0)
-        th00 = tanh_planes(0, z00)
+        xe2(1, 0, 1, b1)
+        z00 = new_z(0)
+        y(0, 0, 0, z00)
         a_quant(0)
+        mix_s(wg[1][0], wraw[1][0], 0)
+        mix_s(wg[1][0], wraw[1][0], 1)
+        for j in range(1, J):
+            y(0, 0, j, z00)
+        b0 = turn2(1, 1, 0)
+        b1 = turn2(1, 1, 1)
         a_quant(1)
-        u(0)
-        xe(1, 1, b)
+        th00 = new_th(0)
+        tanh(z00, th00, 0)
+        xe2(1, 1, 0, b0)
+        xe2(1, 1, 1, b1)
+        mix_s(wg[1][1], wraw[1][1], 0)
+        for j in range(J):
+            u(0, j)
         x_quant(1)
-        for g in range(G):
-            il_g(wg[1][g], wraw[1][g])
-        z10 = y(1, 0)
-        for c in range(2):
-            il(ug[0], up[0], c)
-        ep00 = wt_planes(0, th00)
-        u(1)
-        th10 = tanh_planes(1, z10)
+        mix_s(wg[1][1], wraw[1][1], 1)
+        weigh_v(0, 0, th00, 0)
+        mix_v(ug[0], up[0], 0)
+        z10 = new_z(1)
+        y(1, 0, 0, z10)
+        y(1, 0, 1, z10)
+        u(1, 0)
+        tanh(z00, th00, 1)
+        u(1, 1)
         w_quant(1, 0)
         w_quant(1, 1)
+        y(1, 0, 2, z10)
+        y(1, 0, 3, z10)
+        u(1, 2)
+        mix_v(ug[0], up[0], 1)
+        weigh_v(0, 0, th00, 1)
+        th10 = new_th(1)
+        tanh(z10, th10, 0)
+        u(1, 3)
+        tanh(z10, th10, 1)
+        weigh_g(1, 0, th10, 0)
+        weigh_g(1, 0, th10, 1)
+        z01 = new_z(0)
+        y(0, 1, 0, z01)
+        y(0, 1, 1, z01)
+        mix_v(ug[1], up[1], 0)
+        y(0, 1, 2, z01)
+        y(0, 1, 3, z01)
+        th01 = new_th(0)
+        tanh(z01, th01, 0)
+        tanh(z01, th01, 1)
+        weigh_g(0, 1, th01, 0)
+        weigh_g(0, 1, th01, 1)
+        e_quant(0, 0, 0)
+        e_quant(0, 0, 1)
+        z11 = new_z(1)
+        for j in range(J):
+            y(1, 1, j, z11)
         u_quant(0)
-        eg00 = new_eg(0)
-        for c in range(2):
-            il(eg00, ep00, c)
-        ep10 = wt_planes(1, th10)
-        z01 = y(0, 1)
-        for c in range(2):
-            il(ug[1], up[1], c)
-        for k in range(2):
-            e_quant(0, 0, eg00, k)
-        th01 = tanh_mixed(0, z01)
-        z11 = y(1, 1)
-        eg10 = new_eg(1)
-        for c in range(2):
-            il(eg10, ep10, c)
+        mix_v(ug[1], up[1], 1)
+        th11 = new_th(1)
+        tanh(z11, th11, 0)
+        tanh(z11, th11, 1)
+        e_quant(1, 0, 0)
+        e_quant(1, 0, 1)
         u_quant(1)
-        for k in range(2):
-            e_quant(1, 0, eg10, k)
-        th11 = tanh_mixed(1, z11)
-        eg01 = new_eg(0)
-        for k in range(2):
-            wt_mixed(0, th01, eg01, k)
         for m in range(4):
-            o(0, m, 0, NF, "S", "acc")
-        for k in range(2):
-            e_quant(0, 1, eg01, k)
-        eg11 = new_eg(1)
-        for k in range(2):
-            wt_mixed(1, th11, eg11, k)
-        for k in range(2):
-            e_quant(1, 1, eg11, k)
+            b = acc([P, NF])
+            for h in range(H):
+                o_pass(b, h, m, 0, NF)
+            o_store(b, m, 0, NF, "S")
+        weigh_v(1, 1, th11, 0)
+        e_quant(0, 1, 0)
+        weigh_v(1, 1, th11, 1)
+        e_quant(1, 1, 0)
+        e_quant(0, 1, 1)
+        e_quant(1, 1, 1)
+        banks = {}
         for k in range(2):
             for m in range(4):
-                o(1, m, k * 256, 256, "VS"[m % 2], "tp")
+                banks[m, k] = tp([P, 256]) if k == 0 and m < 3 else acc([P, 256])
+                o_pass(banks[m, k], 0, m, NF + k * 256, 256)
+        for k in range(2):
+            for m in range(4):
+                o_pass(banks[m, k], 1, m, NF + k * 256, 256)
+                o_store(banks[m, k], m, NF + k * 256, 256, "VS"[m % 2])

@@ -59,14 +59,14 @@ def tile_lorafalogcoshgradient_kernel(tc, x_bytes, x_scale, wm, a, target, s, wt
         nc.scalar.dma_start(out=xs_sb[:], in_=x_scale.rearrange("o (g p t) -> p (o g) t", p=P, t=J))
         load_x(0, 0)
         load_x(0, 1)
-        load_x(1, 0)
         load_w(0, 0)
+        load_x(1, 0)
+        nc.sync.dma_start(out=araw[0][:], in_=a_v[0])
         load_x(1, 1)
         load_w(0, 1)
         nc.scalar.dma_start(out=wt_bf[:], in_=wt.rearrange("(h p j) -> p h j", p=P, j=J))
         nc.scalar.dma_start(out=s_bf[:], in_=s.rearrange("(h p j) -> p h j", p=P, j=J))
-        for g in range(G):
-            nc.sync.dma_start(out=araw[g][:], in_=a_v[g])
+        nc.sync.dma_start(out=araw[1][:], in_=a_v[1])
         nc.sync.dma_start(out=traw[0][:], in_=t_v[0])
         load_w(1, 0)
         load_w(1, 1)
@@ -249,102 +249,96 @@ def tile_lorafalogcoshgradient_kernel(tc, x_bytes, x_scale, wm, a, target, s, wt
         xe1(0, 0, b)
         b = turn1(0, 1)
         xe1(0, 1, b)
-        b0 = turn2(0, 1, 0)
-        b1 = turn2(0, 1, 1)
-        cast(1, 0, "S")
-        cast(1, 1, "S")
-        xe2(0, 1, 0, b0)
-        xe2(0, 1, 1, b1)
-        for c in range(2):
-            for g in range(G):
-                mix_s(wg[0][g], wraw[0][g], c)
-        nc.vector.tensor_copy(wt32[:], wt_bf[:])
-        nc.vector.tensor_copy(s32[:], s_bf[:])
+        for j in range(J):
+            cast(1, j, "S")
+        mix_g(wg[0][0], wraw[0][0])
+        for g in range(G):
+            b = turn2(0, 1, g)
+            xe2(0, 1, g, b)
+        for g in range(G):
+            b = turn2(1, 0, g)
+            xe2(1, 0, g, b)
         for g in range(G):
             mix_g(ag[g], araw[g])
-        b0 = turn2(1, 0, 0)
-        b1 = turn2(1, 0, 1)
-        x_quant(0)
-        xe2(1, 0, 0, b0)
-        cast(1, 2, "S")
-        cast(1, 3, "S")
+        nc.vector.tensor_copy(wt32[:], wt_bf[:])
+        nc.vector.tensor_copy(s32[:], s_bf[:])
         w_quant(0, 0)
+        x_quant(0)
+        mix_s(wg[0][1], wraw[0][1], 0)
+        mix_s(wg[0][1], wraw[0][1], 1)
         w_quant(0, 1)
-        xe2(1, 0, 1, b1)
-        z00 = new_z(0)
-        y(0, 0, 0, z00)
-        a_quant(0)
-        mix_s(wg[1][0], wraw[1][0], 0)
-        mix_s(wg[1][0], wraw[1][0], 1)
-        for j in range(1, J):
-            y(0, 0, j, z00)
         b0 = turn2(1, 1, 0)
         b1 = turn2(1, 1, 1)
-        a_quant(1)
+        xe2(1, 1, 0, b0)
+        z00 = new_z(0)
+        y(0, 0, 0, z00)
+        xe2(1, 1, 1, b1)
+        for c in range(2):
+            mix_s(wg[1][0], wraw[1][0], c)
+        for j in range(1, J):
+            y(0, 0, j, z00)
+        mix_s(wg[1][1], wraw[1][1], 0)
+        x_quant(1)
         th00 = new_th(0)
         tanh(z00, th00, 0)
-        xe2(1, 1, 0, b0)
-        xe2(1, 1, 1, b1)
-        mix_s(wg[1][1], wraw[1][1], 0)
-        for j in range(J):
-            u(0, j)
-        x_quant(1)
-        mix_s(wg[1][1], wraw[1][1], 1)
-        weigh_v(0, 0, th00, 0)
-        mix_v(ug[0], up[0], 0)
+        a_quant(0)
+        a_quant(1)
         z10 = new_z(1)
         y(1, 0, 0, z10)
         y(1, 0, 1, z10)
-        u(1, 0)
         tanh(z00, th00, 1)
-        u(1, 1)
+        u(0, 0)
+        mix_s(wg[1][1], wraw[1][1], 1)
+        weigh_v(0, 0, th00, 0)
+        y(1, 0, 2, z10)
+        weigh_v(0, 0, th00, 1)
+        y(1, 0, 3, z10)
+        for j in range(1, J):
+            u(0, j)
         w_quant(1, 0)
         w_quant(1, 1)
-        y(1, 0, 2, z10)
-        y(1, 0, 3, z10)
-        u(1, 2)
-        mix_v(ug[0], up[0], 1)
-        weigh_v(0, 0, th00, 1)
-        th10 = new_th(1)
-        tanh(z10, th10, 0)
-        u(1, 3)
-        tanh(z10, th10, 1)
-        weigh_g(1, 0, th10, 0)
-        weigh_g(1, 0, th10, 1)
-        z01 = new_z(0)
-        y(0, 1, 0, z01)
-        y(0, 1, 1, z01)
-        mix_v(ug[1], up[1], 0)
-        y(0, 1, 2, z01)
-        y(0, 1, 3, z01)
-        th01 = new_th(0)
-        tanh(z01, th01, 0)
-        tanh(z01, th01, 1)
-        weigh_g(0, 1, th01, 0)
-        weigh_g(0, 1, th01, 1)
+        mix_v(ug[0], up[0], 0)
+        for j in range(J):
+            u(1, j)
         e_quant(0, 0, 0)
         e_quant(0, 0, 1)
+        mix_v(ug[0], up[0], 1)
+        th10 = new_th(1)
+        for k in range(2):
+            tanh(z10, th10, k)
+        mix_v(ug[1], up[1], 0)
+        mix_v(ug[1], up[1], 1)
+        for k in range(2):
+            weigh_g(1, 0, th10, k)
+        z01 = new_z(0)
+        for j in range(J):
+            y(0, 1, j, z01)
         z11 = new_z(1)
         for j in range(J):
             y(1, 1, j, z11)
+        th01 = new_th(0)
+        for k in range(2):
+            tanh(z01, th01, k)
+        u_quant(1)
         u_quant(0)
-        mix_v(ug[1], up[1], 1)
-        th11 = new_th(1)
-        tanh(z11, th11, 0)
-        tanh(z11, th11, 1)
         e_quant(1, 0, 0)
         e_quant(1, 0, 1)
-        u_quant(1)
+        th11 = new_th(1)
+        tanh(z11, th11, 0)
+        weigh_v(0, 1, th01, 0)
+        weigh_v(0, 1, th01, 1)
         for m in range(4):
             b = acc([P, NF])
             for h in range(H):
                 o_pass(b, h, m, 0, NF)
             o_store(b, m, 0, NF, "S")
-        weigh_v(1, 1, th11, 0)
+            if m == 1:
+                tanh(z11, th11, 1)
         e_quant(0, 1, 0)
-        weigh_v(1, 1, th11, 1)
-        e_quant(1, 1, 0)
+        weigh_v(1, 1, th11, 0)
         e_quant(0, 1, 1)
+        e_quant(1, 1, 0)
+        weigh_v(1, 1, th11, 1)
         e_quant(1, 1, 1)
         banks = {}
         for k in range(2):

@@ -56,39 +56,47 @@ def tile_lorafalogcoshgradient_kernel(tc, x_bytes, x_scale, wm, a, target, s, wt
         def load_w(f, g):
             nc.sync.dma_start(out=wraw[f][g][:], in_=wm_v[g][:, :, f * NF : (f + 1) * NF])
 
+        def load_a(g):
+            nc.sync.dma_start(out=araw[g][:], in_=a_v[g])
+
         nc.scalar.dma_start(out=xs_sb[:], in_=x_scale.rearrange("o (g p t) -> p (o g) t", p=P, t=J))
-        load_x(0, 0)
-        load_x(0, 1)
-        load_w(0, 0)
-        load_x(1, 0)
-        nc.sync.dma_start(out=araw[0][:], in_=a_v[0])
-        load_x(1, 1)
-        load_w(0, 1)
         nc.scalar.dma_start(out=wt_bf[:], in_=wt.rearrange("(h p j) -> p h j", p=P, j=J))
         nc.scalar.dma_start(out=s_bf[:], in_=s.rearrange("(h p j) -> p h j", p=P, j=J))
-        nc.sync.dma_start(out=araw[1][:], in_=a_v[1])
-        nc.sync.dma_start(out=traw[0][:], in_=t_v[0])
+        for j in range(2):
+            nc.sync.dma_start(out=xb[0][:, j, :], in_=x_v[0][:, j, :])
+        load_x(0, 1)
+        load_x(1, 0)
+        load_w(0, 0)
+        load_a(0)
+        load_w(0, 1)
+        load_x(1, 1)
         load_w(1, 0)
         load_w(1, 1)
+        load_a(1)
+        nc.sync.dma_start(out=traw[0][:], in_=t_v[0])
         nc.sync.dma_start(out=traw[1][:], in_=t_v[1])
 
         warm = sb("warm", [P, 1], F32)
         warm_o = sb("warm_o", [P, 1], F32)
-        nc.vector.memset(warm[:], 0.0)
+        nc.gpsimd.memset(warm[:], 0.0)
         nc.scalar.activation(warm_o[:], warm[:], ACT.Tanh)
         id32 = sb("id32", [P, P], F32)
         make_identity(nc, id32[:])
+        idb = sb("idb", [P, P], BF16)
+        make_identity(nc, idb[:])
+        nc.gpsimd.tensor_copy(wt32[:], wt_bf[:])
+        nc.gpsimd.tensor_copy(s32[:], s_bf[:])
 
         xcast = [[sb(f"xcast{h}_{sp}", [P, 2, D], BF16) for sp in range(2)] for h in range(H)]
-        xg = [[sb(f"xg{h}_{g}", [P, KP, J], BF16) for g in range(G)] for h in range(H)]
-        xq = [[sb(f"xq{h}_{g}", [P, KP], U32) for g in range(G)] for h in range(H)]
-        xsc = [[sb(f"xsc{h}_{g}", [P, KP], U8) for g in range(G)] for h in range(H)]
-        wg = [[sb(f"wg{f}_{g}", [P, NF, J], BF16) for g in range(G)] for f in range(FH)]
-        wq = [[sb(f"wq{f}_{g}", [P, NF], U32) for g in range(G)] for f in range(FH)]
-        wsc = [[sb(f"wsc{f}_{g}", [P, NF], U8) for g in range(G)] for f in range(FH)]
-        ag = [sb(f"ag{g}", [P, R, J], BF16) for g in range(G)]
-        aq = [sb(f"aq{g}", [P, R], U32) for g in range(G)]
-        asc = [sb(f"asc{g}", [P, R], U8) for g in range(G)]
+        xg = [sb(f"xg{h}", [P, G, KP, J], BF16) for h in range(H)]
+        xq = [sb(f"xq{h}", [P, G, KP], U32) for h in range(H)]
+        xsc = [sb(f"xsc{h}", [P, G, KP], U8) for h in range(H)]
+        wg = [sb(f"wg{f}", [P, G, NF, J], BF16) for f in range(FH)]
+        wq = [sb(f"wq{f}", [P, G, NF], U32) for f in range(FH)]
+        wsc = [sb(f"wsc{f}", [P, G, NF], U8) for f in range(FH)]
+        ag = sb("ag", [P, G, R, J], BF16)
+        aq = sb("aq", [P, G, R], U32)
+        asc = sb("asc", [P, G, R], U8)
         up = [sb(f"up{h}", [P, J, R], BF16) for h in range(H)]
         ug = [sb(f"ug{h}", [P, R, J], BF16) for h in range(H)]
         uq = [sb(f"uq{h}", [P, R], U32) for h in range(H)]
@@ -97,14 +105,21 @@ def tile_lorafalogcoshgradient_kernel(tc, x_bytes, x_scale, wm, a, target, s, wt
         eq = [sb(f"eq{h}", [P, F], U32) for h in range(H)]
         esc = [sb(f"esc{h}", [P, F], U8) for h in range(H)]
 
-        def tp(shape):
-            return psum.tile(shape, F32, name="tp", bufs=3)
+        def tp(shape, dt=F32):
+            return psum.tile(shape, dt, name="tp", bufs=3)
 
         def acc(shape):
             return psum.tile(shape, F32, name="acc", bufs=5)
 
         def quant(codes, scales, src):
             nc.vector.quantize_mx(out=codes.bitcast(FP8X4), scales=scales, in_=src.rearrange("p n j -> p (n j)"))
+
+        def quant_both(codes, scales, src):
+            nc.vector.quantize_mx(
+                out=codes[:].rearrange("p g n -> p (g n)").bitcast(FP8X4),
+                scales=scales[:].rearrange("p g n -> p (g n)"),
+                in_=src[:].rearrange("p g n j -> p (g n j)"),
+            )
 
         def mx(o, lq, ls, rq, rs, start, stop):
             nc.tensor.matmul_mx(
@@ -119,6 +134,15 @@ def tile_lorafalogcoshgradient_kernel(tc, x_bytes, x_scale, wm, a, target, s, wt
             else:
                 nc.scalar.copy(dst, src)
 
+        def cast_half(h, j, g, eng):
+            ds = slice(g * KP, (g + 1) * KP)
+            src = xb[h][:, j, ds].bitcast(FP8)
+            dst = xcast[h][j // 2][:, j % 2, ds]
+            if eng == "V":
+                nc.vector.tensor_copy(dst, src)
+            else:
+                nc.scalar.copy(dst, src)
+
         def words(h, j, g, u):
             w = xcast[h][j // 2][:, j % 2, :].bitcast(F32)
             lo = g * 2 * P + u
@@ -126,7 +150,7 @@ def tile_lorafalogcoshgradient_kernel(tc, x_bytes, x_scale, wm, a, target, s, wt
 
         def x_exit(h, g, bank_view, n0, n):
             xin = bank_view.rearrange("p u n -> p (u n)").bitcast(BF16).rearrange("p (u n e) -> p n u e", u=2, e=2)
-            dst = xg[h][g][:, n0 : n0 + n, :].rearrange("p n (u e) -> p n u e", u=2)
+            dst = xg[h][:, g][:, n0 : n0 + n, :].rearrange("p n (u e) -> p n u e", u=2)
             sc = xs_sb[:, g, :].rearrange("p (u e) -> p u e", u=2).unsqueeze(1).to_broadcast([P, n, 2, 2])
             nc.vector.tensor_tensor(dst, xin, sc, ALU.mult)
 
@@ -152,8 +176,7 @@ def tile_lorafalogcoshgradient_kernel(tc, x_bytes, x_scale, wm, a, target, s, wt
             x_exit(h, g, bank[:], 2 * P * sp, 2 * P)
 
         def x_quant(h):
-            for g in range(G):
-                quant(xq[h][g][:], xsc[h][g][:], xg[h][g][:])
+            quant_both(xq[h], xsc[h], xg[h])
 
         def half(c):
             return slice(c * 256, (c + 1) * 256)
@@ -168,9 +191,21 @@ def tile_lorafalogcoshgradient_kernel(tc, x_bytes, x_scale, wm, a, target, s, wt
             d, q = by4(dst[:, half(c), :], src[:, :, half(c)])
             nc.scalar.copy(d, q)
 
-        def mix_v(dst, src, c):
-            d, q = by4(dst[:, half(c), :], src[:, :, half(c)])
-            nc.vector.tensor_copy(d, q)
+        def il(src, c):
+            bank = tp([P, 256, J], BF16)
+            for q in range(2):
+                lo = c * 256 + q * P
+                nc.tensor.matmul(
+                    bank[:, q * P : (q + 1) * P, :].rearrange("p n j -> p j n"),
+                    lhsT=idb[:],
+                    rhs=src[:, :, lo : lo + P],
+                    start=True,
+                    stop=True,
+                )
+            return bank
+
+        def ix(dst, c, bank):
+            nc.scalar.copy(dst[:, half(c), :], bank[:])
 
         def mix_g(dst, src):
             for c in range(4):
@@ -180,23 +215,20 @@ def tile_lorafalogcoshgradient_kernel(tc, x_bytes, x_scale, wm, a, target, s, wt
                 )
 
         def w_quant(f, g):
-            quant(wq[f][g][:], wsc[f][g][:], wg[f][g][:])
-
-        def a_quant(g):
-            quant(aq[g][:], asc[g][:], ag[g][:])
+            quant(wq[f][:, g, :], wsc[f][:, g, :], wg[f][:, g])
 
         def u(h, j):
             bank = acc([P, R])
             ms = slice(j * P, (j + 1) * P)
             for g in range(G):
-                mx(bank[:], xq[h][g][:, ms], xsc[h][g][:, ms], aq[g][:], asc[g][:], g == 0, g == G - 1)
+                mx(bank[:], xq[h][:, g, ms], xsc[h][:, g, ms], aq[:, g, :], asc[:, g, :], g == 0, g == G - 1)
             nc.scalar.activation(up[h][:, j, :], bank[:], ACT.Copy, scale=s32[:, h, j : j + 1])
 
         def u_quant(h):
             quant(uq[h][:], usc[h][:], ug[h][:])
 
-        def new_z(h):
-            return sb(f"z{h}", [P, J, NF], F32)
+        def new_z(n):
+            return sb(f"z{n}", [P, J, NF], F32)
 
         def new_th(h):
             return sb(f"th{h}", [P, NF, J], F32)
@@ -205,7 +237,7 @@ def tile_lorafalogcoshgradient_kernel(tc, x_bytes, x_scale, wm, a, target, s, wt
             bank = acc([P, NF])
             ms = slice(j * P, (j + 1) * P)
             for g in range(G):
-                mx(bank[:], xq[h][g][:, ms], xsc[h][g][:, ms], wq[f][g][:], wsc[f][g][:], g == 0, g == G - 1)
+                mx(bank[:], xq[h][:, g, ms], xsc[h][:, g, ms], wq[f][:, g, :], wsc[f][:, g, :], g == 0, g == G - 1)
             nc.vector.tensor_tensor(z[:, j, :], bank[:], traw[h][:, j, f * NF : (f + 1) * NF], ALU.subtract)
 
         def tanh(z, th, k):
@@ -220,9 +252,16 @@ def tile_lorafalogcoshgradient_kernel(tc, x_bytes, x_scale, wm, a, target, s, wt
         def weigh_v(h, f, th, k):
             weigh(nc.vector, h, f, th, k * 256, 256)
 
+        def weigh_v2(h, f, th):
+            weigh(nc.vector, h, f, th, 0, NF)
+
         def weigh_g(h, f, th, k):
             for q in range(2):
                 weigh(nc.gpsimd, h, f, th, k * 256 + q * P, P)
+
+        def e_quant2(h, f):
+            cs = slice(f * NF, (f + 1) * NF)
+            quant(eq[h][:, cs], esc[h][:, cs], eg[h][f][:])
 
         def e_quant(h, f, k):
             cs = slice(f * NF + k * 256, f * NF + (k + 1) * 256)
@@ -241,111 +280,154 @@ def tile_lorafalogcoshgradient_kernel(tc, x_bytes, x_scale, wm, a, target, s, wt
                 nc.scalar.activation(res[:], bank[:], ACT.Copy, scale=1.0 / 32.0)
             nc.sync.dma_start(out=out[m * P : (m + 1) * P, c0 : c0 + n], in_=res[:])
 
-        cast(0, 0, "V")
-        cast(0, 1, "S")
-        cast(0, 2, "V")
+        cast_half(0, 0, 0, "V")
+        cast_half(0, 0, 1, "S")
+        cast_half(0, 1, 0, "V")
+        cast_half(0, 1, 1, "S")
+        cast(0, 2, "S")
         cast(0, 3, "S")
-        b = turn1(0, 0)
-        xe1(0, 0, b)
-        b = turn1(0, 1)
-        xe1(0, 1, b)
-        for j in range(J):
-            cast(1, j, "S")
-        mix_g(wg[0][0], wraw[0][0])
-        for g in range(G):
-            b = turn2(0, 1, g)
-            xe2(0, 1, g, b)
-        for g in range(G):
-            b = turn2(1, 0, g)
-            xe2(1, 0, g, b)
-        for g in range(G):
-            mix_g(ag[g], araw[g])
-        nc.vector.tensor_copy(wt32[:], wt_bf[:])
-        nc.vector.tensor_copy(s32[:], s_bf[:])
-        w_quant(0, 0)
+        b00 = turn1(0, 0)
+        xe1(0, 0, b00)
+        b01 = turn1(0, 1)
+        xe1(0, 1, b01)
+        cast(1, 0, "S")
+        cast(1, 1, "S")
+        mix_g(wg[0][:, 0], wraw[0][0])
+        mix_g(ag[:, 0], araw[0])
+        mix_g(ag[:, 1], araw[1])
+        b010 = turn2(0, 1, 0)
+        xe2(0, 1, 0, b010)
+        b011 = turn2(0, 1, 1)
+        xe2(0, 1, 1, b011)
+        b100 = turn2(1, 0, 0)
+        xe2(1, 0, 0, b100)
+        b101 = turn2(1, 0, 1)
+        xe2(1, 0, 1, b101)
+        mix_s(wg[0][:, 1], wraw[0][1], 0)
+        cast(1, 2, "S")
+        cast(1, 3, "S")
+        mix_s(wg[0][:, 1], wraw[0][1], 1)
         x_quant(0)
-        mix_s(wg[0][1], wraw[0][1], 0)
-        mix_s(wg[0][1], wraw[0][1], 1)
+        w_quant(0, 0)
         w_quant(0, 1)
-        b0 = turn2(1, 1, 0)
-        b1 = turn2(1, 1, 1)
-        xe2(1, 1, 0, b0)
+        b110 = turn2(1, 1, 0)
+        xe2(1, 1, 0, b110)
+        b111 = turn2(1, 1, 1)
+        xe2(1, 1, 1, b111)
+        mix_s(wg[1][:, 0], wraw[1][0], 0)
+        mix_s(wg[1][:, 0], wraw[1][0], 1)
+        mix_s(wg[1][:, 1], wraw[1][1], 0)
+        mix_s(wg[1][:, 1], wraw[1][1], 1)
         z00 = new_z(0)
         y(0, 0, 0, z00)
-        xe2(1, 1, 1, b1)
-        for c in range(2):
-            mix_s(wg[1][0], wraw[1][0], c)
-        for j in range(1, J):
-            y(0, 0, j, z00)
-        mix_s(wg[1][1], wraw[1][1], 0)
+        y(0, 0, 1, z00)
         x_quant(1)
+        y(0, 0, 2, z00)
+        y(0, 0, 3, z00)
+        quant_both(aq, asc, ag)
         th00 = new_th(0)
         tanh(z00, th00, 0)
-        a_quant(0)
-        a_quant(1)
+        tanh(z00, th00, 1)
         z10 = new_z(1)
         y(1, 0, 0, z10)
         y(1, 0, 1, z10)
-        tanh(z00, th00, 1)
-        u(0, 0)
-        mix_s(wg[1][1], wraw[1][1], 1)
-        weigh_v(0, 0, th00, 0)
         y(1, 0, 2, z10)
-        weigh_v(0, 0, th00, 1)
         y(1, 0, 3, z10)
-        for j in range(1, J):
-            u(0, j)
-        w_quant(1, 0)
-        w_quant(1, 1)
-        mix_v(ug[0], up[0], 0)
-        for j in range(J):
-            u(1, j)
-        e_quant(0, 0, 0)
-        e_quant(0, 0, 1)
-        mix_v(ug[0], up[0], 1)
+        quant_both(wq[1], wsc[1], wg[1])
+        weigh_v2(0, 0, th00)
+        u(0, 0)
+        u(0, 1)
+        u(0, 2)
+        u(0, 3)
+        u(1, 0)
+        u(1, 1)
+        u(1, 2)
         th10 = new_th(1)
-        for k in range(2):
-            tanh(z10, th10, k)
-        mix_v(ug[1], up[1], 0)
-        mix_v(ug[1], up[1], 1)
-        for k in range(2):
-            weigh_g(1, 0, th10, k)
+        tanh(z10, th10, 0)
         z01 = new_z(0)
-        for j in range(J):
-            y(0, 1, j, z01)
-        z11 = new_z(1)
-        for j in range(J):
-            y(1, 1, j, z11)
+        y(0, 1, 0, z01)
+        e_quant2(0, 0)
+        u(1, 3)
+        tanh(z10, th10, 1)
+        weigh_g(1, 0, th10, 0)
+        weigh_g(1, 0, th10, 1)
+        i00 = il(up[0], 0)
+        ix(ug[0], 0, i00)
+        y(0, 1, 1, z01)
+        y(0, 1, 2, z01)
+        y(0, 1, 3, z01)
         th01 = new_th(0)
-        for k in range(2):
-            tanh(z01, th01, k)
-        u_quant(1)
-        u_quant(0)
-        e_quant(1, 0, 0)
-        e_quant(1, 0, 1)
+        tanh(z01, th01, 0)
+        tanh(z01, th01, 1)
+        z11 = new_z(2)
+        y(1, 1, 0, z11)
+        y(1, 1, 1, z11)
+        y(1, 1, 2, z11)
+        y(1, 1, 3, z11)
         th11 = new_th(1)
         tanh(z11, th11, 0)
+        i01 = il(up[0], 1)
+        ix(ug[0], 1, i01)
+        i10 = il(up[1], 0)
+        ix(ug[1], 0, i10)
+        i11 = il(up[1], 1)
+        ix(ug[1], 1, i11)
+        tanh(z11, th11, 1)
         weigh_v(0, 1, th01, 0)
+        e_quant2(1, 0)
         weigh_v(0, 1, th01, 1)
-        for m in range(4):
-            b = acc([P, NF])
-            for h in range(H):
-                o_pass(b, h, m, 0, NF)
-            o_store(b, m, 0, NF, "S")
-            if m == 1:
-                tanh(z11, th11, 1)
-        e_quant(0, 1, 0)
+        u_quant(0)
+        u_quant(1)
+        o0 = acc([P, NF])
+        o_pass(o0, 0, 0, 0, NF)
+        o_pass(o0, 1, 0, 0, NF)
+        o_store(o0, 0, 0, NF, "S")
+        o1 = acc([P, NF])
+        o_pass(o1, 0, 1, 0, NF)
+        o_pass(o1, 1, 1, 0, NF)
+        o_store(o1, 1, 0, NF, "S")
+        o2 = acc([P, NF])
+        o_pass(o2, 0, 2, 0, NF)
+        o_pass(o2, 1, 2, 0, NF)
+        o_store(o2, 2, 0, NF, "S")
+        o3 = acc([P, NF])
+        o_pass(o3, 0, 3, 0, NF)
+        o_pass(o3, 1, 3, 0, NF)
+        o_store(o3, 3, 0, NF, "S")
         weigh_v(1, 1, th11, 0)
-        e_quant(0, 1, 1)
+        e_quant2(0, 1)
         e_quant(1, 1, 0)
         weigh_v(1, 1, th11, 1)
+        p00 = tp([P, 256])
+        o_pass(p00, 0, 0, NF, 256)
+        p10 = tp([P, 256])
+        o_pass(p10, 0, 1, NF, 256)
+        p20 = tp([P, 256])
+        o_pass(p20, 0, 2, NF, 256)
+        p30 = acc([P, 256])
+        o_pass(p30, 0, 3, NF, 256)
+        p01 = acc([P, 256])
+        o_pass(p01, 0, 0, NF + 256, 256)
+        p11 = acc([P, 256])
+        o_pass(p11, 0, 1, NF + 256, 256)
+        p21 = acc([P, 256])
+        o_pass(p21, 0, 2, NF + 256, 256)
+        p31 = acc([P, 256])
+        o_pass(p31, 0, 3, NF + 256, 256)
+        o_pass(p00, 1, 0, NF, 256)
+        o_store(p00, 0, NF, 256, "V")
         e_quant(1, 1, 1)
-        banks = {}
-        for k in range(2):
-            for m in range(4):
-                banks[m, k] = tp([P, 256]) if k == 0 and m < 3 else acc([P, 256])
-                o_pass(banks[m, k], 0, m, NF + k * 256, 256)
-        for k in range(2):
-            for m in range(4):
-                o_pass(banks[m, k], 1, m, NF + k * 256, 256)
-                o_store(banks[m, k], m, NF + k * 256, 256, "VS"[m % 2])
+        o_pass(p10, 1, 1, NF, 256)
+        o_store(p10, 1, NF, 256, "S")
+        o_pass(p20, 1, 2, NF, 256)
+        o_store(p20, 2, NF, 256, "V")
+        o_pass(p30, 1, 3, NF, 256)
+        o_store(p30, 3, NF, 256, "S")
+        o_pass(p01, 1, 0, NF + 256, 256)
+        o_store(p01, 0, NF + 256, 256, "V")
+        o_pass(p11, 1, 1, NF + 256, 256)
+        o_store(p11, 1, NF + 256, 256, "S")
+        o_pass(p21, 1, 2, NF + 256, 256)
+        o_store(p21, 2, NF + 256, 256, "V")
+        o_pass(p31, 1, 3, NF + 256, 256)
+        o_store(p31, 3, NF + 256, 256, "S")

from contextlib import ExitStack

import concourse.mybir as mybir
from concourse.masks import make_identity

T, D, F, R = 1024, 1024, 1024, 512
P = 128
J = 4
KP = P * J
H = T // KP
G = D // KP
NF = 512
FH = F // NF

FLOPS = 2 * T * D * F + 2 * T * D * R + 2 * T * R * F

F32 = mybir.dt.float32
BF16 = mybir.dt.bfloat16
U32 = mybir.dt.uint32
U8 = mybir.dt.uint8
FP8 = mybir.dt.float8_e4m3fn
FP8X4 = mybir.dt.float8_e4m3fn_x4
ALU = mybir.AluOpType
ACT = mybir.ActivationFunctionType


def tile_lorafalogcoshgradient_kernel(tc, x_bytes, x_scale, wm, a, target, s, wt, out):
    nc = tc.nc
    with ExitStack() as ctx:
        keep = ctx.enter_context(tc.tile_pool(name="keep", bufs=1))
        psum = ctx.enter_context(tc.psum_pool(name="psum", bufs=1))
        ctx.enter_context(tc.manual_schedule())

        def sb(name, shape, dt):
            return keep.tile(shape, dt, name=name, align_bytes=64)

        xs_sb = sb("xs_sb", [P, G, J], F32)
        s_bf = sb("s_bf", [P, H, J], BF16)
        wt_bf = sb("wt_bf", [P, H, J], BF16)
        s32 = sb("s32", [P, H, J], F32)
        wt32 = sb("wt32", [P, H, J], F32)
        xb = [sb(f"xb{h}", [P, J, D], U8) for h in range(H)]
        wraw = [[sb(f"wraw{f}_{g}", [P, J, NF], BF16) for g in range(G)] for f in range(FH)]
        araw = [sb(f"araw{g}", [P, J, R], BF16) for g in range(G)]
        traw = [sb(f"traw{h}", [P, J, F], BF16) for h in range(H)]

        x_v = x_bytes.rearrange("(h p j) d -> h p j d", p=P, j=J)
        wm_v = wm.rearrange("(g p j) f -> g p j f", p=P, j=J)
        a_v = a.rearrange("(g p j) r -> g p j r", p=P, j=J)
        t_v = target.rearrange("(h p j) f -> h p j f", p=P, j=J)

        def load_x(h, sp):
            js = slice(2 * sp, 2 * sp + 2)
            nc.sync.dma_start(out=xb[h][:, js, :], in_=x_v[h][:, js, :])

        def load_w(f, g):
            nc.sync.dma_start(out=wraw[f][g][:], in_=wm_v[g][:, :, f * NF : (f + 1) * NF])

        def load_a(g):
            nc.sync.dma_start(out=araw[g][:], in_=a_v[g])

        nc.scalar.dma_start(out=xs_sb[:], in_=x_scale.rearrange("o (g p t) -> p (o g) t", p=P, t=J))
        nc.scalar.dma_start(out=wt_bf[:], in_=wt.rearrange("(h p j) -> p h j", p=P, j=J))
        nc.scalar.dma_start(out=s_bf[:], in_=s.rearrange("(h p j) -> p h j", p=P, j=J))
        for j in range(2):
            nc.sync.dma_start(out=xb[0][:, j, :], in_=x_v[0][:, j, :])
        load_x(0, 1)
        load_x(1, 0)
        load_w(0, 0)
        load_a(0)
        load_w(0, 1)
        load_x(1, 1)
        load_w(1, 0)
        load_w(1, 1)
        load_a(1)
        nc.sync.dma_start(out=traw[0][:], in_=t_v[0])
        nc.sync.dma_start(out=traw[1][:], in_=t_v[1])

        warm = sb("warm", [P, 1], F32)
        warm_o = sb("warm_o", [P, 1], F32)
        nc.gpsimd.memset(warm[:], 0.0)
        nc.scalar.activation(warm_o[:], warm[:], ACT.Tanh)
        id32 = sb("id32", [P, P], F32)
        make_identity(nc, id32[:])
        idb = sb("idb", [P, P], BF16)
        make_identity(nc, idb[:])
        nc.gpsimd.tensor_copy(wt32[:], wt_bf[:])
        nc.gpsimd.tensor_copy(s32[:], s_bf[:])

        xcast = [[sb(f"xcast{h}_{sp}", [P, 2, D], BF16) for sp in range(2)] for h in range(H)]
        xg = [sb(f"xg{h}", [P, G, KP, J], BF16) for h in range(H)]
        xq = [sb(f"xq{h}", [P, G, KP], U32) for h in range(H)]
        xsc = [sb(f"xsc{h}", [P, G, KP], U8) for h in range(H)]
        wg = [sb(f"wg{f}", [P, G, NF, J], BF16) for f in range(FH)]
        wq = [sb(f"wq{f}", [P, G, NF], U32) for f in range(FH)]
        wsc = [sb(f"wsc{f}", [P, G, NF], U8) for f in range(FH)]
        ag = sb("ag", [P, G, R, J], BF16)
        aq = sb("aq", [P, G, R], U32)
        asc = sb("asc", [P, G, R], U8)
        up = [sb(f"up{h}", [P, J, R], BF16) for h in range(H)]
        ug = [sb(f"ug{h}", [P, R, J], BF16) for h in range(H)]
        uq = [sb(f"uq{h}", [P, R], U32) for h in range(H)]
        usc = [sb(f"usc{h}", [P, R], U8) for h in range(H)]
        eg = [[sb(f"eg{h}_{f}", [P, NF, J], BF16) for f in range(FH)] for h in range(H)]
        eq = [sb(f"eq{h}", [P, F], U32) for h in range(H)]
        esc = [sb(f"esc{h}", [P, F], U8) for h in range(H)]

        def tp(shape, dt=F32):
            return psum.tile(shape, dt, name="tp", bufs=3)

        def acc(shape):
            return psum.tile(shape, F32, name="acc", bufs=5)

        def quant(codes, scales, src):
            nc.vector.quantize_mx(out=codes.bitcast(FP8X4), scales=scales, in_=src.rearrange("p n j -> p (n j)"))

        def quant_both(codes, scales, src):
            nc.vector.quantize_mx(
                out=codes[:].rearrange("p g n -> p (g n)").bitcast(FP8X4),
                scales=scales[:].rearrange("p g n -> p (g n)"),
                in_=src[:].rearrange("p g n j -> p (g n j)"),
            )

        def mx(o, lq, ls, rq, rs, start, stop):
            nc.tensor.matmul_mx(
                out=o, lhsT=lq.bitcast(FP8X4), lhsT_scale=ls, rhs=rq.bitcast(FP8X4), rhs_scale=rs, start=start, stop=stop
            )

        def cast(h, j, eng):
            src = xb[h][:, j, :].bitcast(FP8)
            dst = xcast[h][j // 2][:, j % 2, :]
            if eng == "V":
                nc.vector.tensor_copy(dst, src)
            else:
                nc.scalar.copy(dst, src)

        def cast_half(h, j, g, eng):
            ds = slice(g * KP, (g + 1) * KP)
            src = xb[h][:, j, ds].bitcast(FP8)
            dst = xcast[h][j // 2][:, j % 2, ds]
            if eng == "V":
                nc.vector.tensor_copy(dst, src)
            else:
                nc.scalar.copy(dst, src)

        def words(h, j, g, u):
            w = xcast[h][j // 2][:, j % 2, :].bitcast(F32)
            lo = g * 2 * P + u
            return w[:, lo : lo + 2 * P - 1 : 2]

        def x_exit(h, g, bank_view, n0, n):
            xin = bank_view.rearrange("p u n -> p (u n)").bitcast(BF16).rearrange("p (u n e) -> p n u e", u=2, e=2)
            dst = xg[h][:, g][:, n0 : n0 + n, :].rearrange("p n (u e) -> p n u e", u=2)
            sc = xs_sb[:, g, :].rearrange("p (u e) -> p u e", u=2).unsqueeze(1).to_broadcast([P, n, 2, 2])
            nc.vector.tensor_tensor(dst, xin, sc, ALU.mult)

        def turn1(h, j):
            bank = tp([P, G, 2, P])
            for g in range(G):
                for u in range(2):
                    nc.tensor.transpose(bank[:, g, u, :], words(h, j, g, u), id32[:])
            return bank

        def xe1(h, j, bank):
            for g in range(G):
                x_exit(h, g, bank[:, g, :, :], j * P, P)

        def turn2(h, sp, g):
            bank = tp([P, 2, 2 * P])
            for j in range(2):
                for u in range(2):
                    nc.tensor.transpose(bank[:, u, j * P : (j + 1) * P], words(h, 2 * sp + j, g, u), id32[:])
            return bank

        def xe2(h, sp, g, bank):
            x_exit(h, g, bank[:], 2 * P * sp, 2 * P)

        def x_quant(h):
            quant_both(xq[h], xsc[h], xg[h])

        def half(c):
            return slice(c * 256, (c + 1) * 256)

        def by4(dst, src):
            return (
                dst.rearrange("p (c i) t -> p c t i", i=4),
                src.rearrange("p t (c i) -> p c t i", i=4),
            )

        def mix_s(dst, src, c):
            d, q = by4(dst[:, half(c), :], src[:, :, half(c)])
            nc.scalar.copy(d, q)

        def il(src, c):
            bank = tp([P, 256, J], BF16)
            for q in range(2):
                lo = c * 256 + q * P
                nc.tensor.matmul(
                    bank[:, q * P : (q + 1) * P, :].rearrange("p n j -> p j n"),
                    lhsT=idb[:],
                    rhs=src[:, :, lo : lo + P],
                    start=True,
                    stop=True,
                )
            return bank

        def ix(dst, c, bank):
            nc.scalar.copy(dst[:, half(c), :], bank[:])

        def mix_g(dst, src):
            for c in range(4):
                cs = slice(c * P, (c + 1) * P)
                nc.gpsimd.tensor_scalar(
                    dst[:, cs, :], src[:, :, cs].rearrange("p j n -> p n j"), 1.0, 0.0, ALU.mult, ALU.add
                )

        def w_quant(f, g):
            quant(wq[f][:, g, :], wsc[f][:, g, :], wg[f][:, g])

        def u(h, j):
            bank = acc([P, R])
            ms = slice(j * P, (j + 1) * P)
            for g in range(G):
                mx(bank[:], xq[h][:, g, ms], xsc[h][:, g, ms], aq[:, g, :], asc[:, g, :], g == 0, g == G - 1)
            nc.scalar.activation(up[h][:, j, :], bank[:], ACT.Copy, scale=s32[:, h, j : j + 1])

        def u_quant(h):
            quant(uq[h][:], usc[h][:], ug[h][:])

        def new_z(n):
            return sb(f"z{n}", [P, J, NF], F32)

        def new_th(h):
            return sb(f"th{h}", [P, NF, J], F32)

        def y(h, f, j, z):
            bank = acc([P, NF])
            ms = slice(j * P, (j + 1) * P)
            for g in range(G):
                mx(bank[:], xq[h][:, g, ms], xsc[h][:, g, ms], wq[f][:, g, :], wsc[f][:, g, :], g == 0, g == G - 1)
            nc.vector.tensor_tensor(z[:, j, :], bank[:], traw[h][:, j, f * NF : (f + 1) * NF], ALU.subtract)

        def tanh(z, th, k):
            nc.scalar.activation(th[:, half(k), :], z[:, :, half(k)].rearrange("p j n -> p n j"), ACT.Tanh)

        def weigh(eng, h, f, th, c0, n):
            cs = slice(c0, c0 + n)
            eng.tensor_tensor(
                eg[h][f][:, cs, :], th[:, cs, :], wt32[:, h, :].unsqueeze(1).to_broadcast([P, n, J]), ALU.mult
            )

        def weigh_v(h, f, th, k):
            weigh(nc.vector, h, f, th, k * 256, 256)

        def weigh_v2(h, f, th):
            weigh(nc.vector, h, f, th, 0, NF)

        def weigh_g(h, f, th, k):
            for q in range(2):
                weigh(nc.gpsimd, h, f, th, k * 256 + q * P, P)

        def e_quant2(h, f):
            cs = slice(f * NF, (f + 1) * NF)
            quant(eq[h][:, cs], esc[h][:, cs], eg[h][f][:])

        def e_quant(h, f, k):
            cs = slice(f * NF + k * 256, f * NF + (k + 1) * 256)
            quant(eq[h][:, cs], esc[h][:, cs], eg[h][f][:, half(k), :])

        def o_pass(bank, h, m, c0, n):
            ms = slice(m * P, (m + 1) * P)
            cs = slice(c0, c0 + n)
            mx(bank[:], uq[h][:, ms], usc[h][:, ms], eq[h][:, cs], esc[h][:, cs], h == 0, h == H - 1)

        def o_store(bank, m, c0, n, eng):
            res = sb(f"res{m}_{c0}", [P, n], F32)
            if eng == "V":
                nc.vector.tensor_scalar(res[:], bank[:], 1.0 / 32.0, None, ALU.mult)
            else:
                nc.scalar.activation(res[:], bank[:], ACT.Copy, scale=1.0 / 32.0)
            nc.sync.dma_start(out=out[m * P : (m + 1) * P, c0 : c0 + n], in_=res[:])

        cast_half(0, 0, 0, "V")
        cast_half(0, 0, 1, "S")
        cast_half(0, 1, 0, "V")
        cast_half(0, 1, 1, "S")
        cast(0, 2, "S")
        cast(0, 3, "S")
        b00 = turn1(0, 0)
        xe1(0, 0, b00)
        b01 = turn1(0, 1)
        xe1(0, 1, b01)
        cast(1, 0, "S")
        cast(1, 1, "S")
        mix_g(wg[0][:, 0], wraw[0][0])
        mix_g(ag[:, 0], araw[0])
        mix_g(ag[:, 1], araw[1])
        b010 = turn2(0, 1, 0)
        xe2(0, 1, 0, b010)
        b011 = turn2(0, 1, 1)
        xe2(0, 1, 1, b011)
        b100 = turn2(1, 0, 0)
        xe2(1, 0, 0, b100)
        b101 = turn2(1, 0, 1)
        xe2(1, 0, 1, b101)
        mix_s(wg[0][:, 1], wraw[0][1], 0)
        cast(1, 2, "S")
        cast(1, 3, "S")
        mix_s(wg[0][:, 1], wraw[0][1], 1)
        x_quant(0)
        w_quant(0, 0)
        w_quant(0, 1)
        b110 = turn2(1, 1, 0)
        xe2(1, 1, 0, b110)
        b111 = turn2(1, 1, 1)
        xe2(1, 1, 1, b111)
        mix_s(wg[1][:, 0], wraw[1][0], 0)
        mix_s(wg[1][:, 0], wraw[1][0], 1)
        mix_s(wg[1][:, 1], wraw[1][1], 0)
        mix_s(wg[1][:, 1], wraw[1][1], 1)
        z00 = new_z(0)
        y(0, 0, 0, z00)
        y(0, 0, 1, z00)
        x_quant(1)
        y(0, 0, 2, z00)
        y(0, 0, 3, z00)
        quant_both(aq, asc, ag)
        th00 = new_th(0)
        tanh(z00, th00, 0)
        tanh(z00, th00, 1)
        z10 = new_z(1)
        y(1, 0, 0, z10)
        y(1, 0, 1, z10)
        y(1, 0, 2, z10)
        y(1, 0, 3, z10)
        quant_both(wq[1], wsc[1], wg[1])
        weigh_v2(0, 0, th00)
        u(0, 0)
        u(0, 1)
        u(0, 2)
        u(0, 3)
        u(1, 0)
        u(1, 1)
        u(1, 2)
        th10 = new_th(1)
        tanh(z10, th10, 0)
        z01 = new_z(0)
        y(0, 1, 0, z01)
        e_quant2(0, 0)
        u(1, 3)
        tanh(z10, th10, 1)
        weigh_g(1, 0, th10, 0)
        weigh_g(1, 0, th10, 1)
        i00 = il(up[0], 0)
        ix(ug[0], 0, i00)
        y(0, 1, 1, z01)
        y(0, 1, 2, z01)
        y(0, 1, 3, z01)
        th01 = new_th(0)
        tanh(z01, th01, 0)
        tanh(z01, th01, 1)
        z11 = new_z(2)
        y(1, 1, 0, z11)
        y(1, 1, 1, z11)
        y(1, 1, 2, z11)
        y(1, 1, 3, z11)
        th11 = new_th(1)
        tanh(z11, th11, 0)
        i01 = il(up[0], 1)
        ix(ug[0], 1, i01)
        i10 = il(up[1], 0)
        ix(ug[1], 0, i10)
        i11 = il(up[1], 1)
        ix(ug[1], 1, i11)
        tanh(z11, th11, 1)
        weigh_v(0, 1, th01, 0)
        e_quant2(1, 0)
        weigh_v(0, 1, th01, 1)
        u_quant(0)
        u_quant(1)
        o0 = acc([P, NF])
        o_pass(o0, 0, 0, 0, NF)
        o_pass(o0, 1, 0, 0, NF)
        o_store(o0, 0, 0, NF, "S")
        o1 = acc([P, NF])
        o_pass(o1, 0, 1, 0, NF)
        o_pass(o1, 1, 1, 0, NF)
        o_store(o1, 1, 0, NF, "S")
        o2 = acc([P, NF])
        o_pass(o2, 0, 2, 0, NF)
        o_pass(o2, 1, 2, 0, NF)
        o_store(o2, 2, 0, NF, "S")
        o3 = acc([P, NF])
        o_pass(o3, 0, 3, 0, NF)
        o_pass(o3, 1, 3, 0, NF)
        o_store(o3, 3, 0, NF, "S")
        weigh_v(1, 1, th11, 0)
        e_quant2(0, 1)
        e_quant(1, 1, 0)
        weigh_v(1, 1, th11, 1)
        p00 = tp([P, 256])
        o_pass(p00, 0, 0, NF, 256)
        p10 = tp([P, 256])
        o_pass(p10, 0, 1, NF, 256)
        p20 = tp([P, 256])
        o_pass(p20, 0, 2, NF, 256)
        p30 = acc([P, 256])
        o_pass(p30, 0, 3, NF, 256)
        p01 = acc([P, 256])
        o_pass(p01, 0, 0, NF + 256, 256)
        p11 = acc([P, 256])
        o_pass(p11, 0, 1, NF + 256, 256)
        p21 = acc([P, 256])
        o_pass(p21, 0, 2, NF + 256, 256)
        p31 = acc([P, 256])
        o_pass(p31, 0, 3, NF + 256, 256)
        o_pass(p00, 1, 0, NF, 256)
        o_store(p00, 0, NF, 256, "V")
        e_quant(1, 1, 1)
        o_pass(p10, 1, 1, NF, 256)
        o_store(p10, 1, NF, 256, "S")
        o_pass(p20, 1, 2, NF, 256)
        o_store(p20, 2, NF, 256, "V")
        o_pass(p30, 1, 3, NF, 256)
        o_store(p30, 3, NF, 256, "S")
        o_pass(p01, 1, 0, NF + 256, 256)
        o_store(p01, 0, NF + 256, 256, "V")
        o_pass(p11, 1, 1, NF + 256, 256)
        o_store(p11, 1, NF + 256, 256, "S")
        o_pass(p21, 1, 2, NF + 256, 256)
        o_store(p21, 2, NF + 256, 256, "V")
        o_pass(p31, 1, 3, NF + 256, 256)
        o_store(p31, 3, NF + 256, 256, "S")
